import numpy as np
import ml_dtypes


def mxq(x, axis, fmt="e4m3"):
    dtype, down = {"e4m3": (ml_dtypes.float8_e4m3fn, 7), "e5m2": (ml_dtypes.float8_e5m2, 14)}[fmt]
    v = np.moveaxis(np.asarray(x, np.float32).astype(ml_dtypes.bfloat16).astype(np.float64), axis, -1)
    blocks = v.reshape(v.shape[:-1] + (-1, 32))
    amax = np.abs(blocks).max(-1, keepdims=True)
    byte = np.maximum(np.where(amax > 0, np.frexp(amax)[1] - 1 + 127, 0) - down, 1)
    scale = np.exp2(byte - 127.0)
    codes = (blocks / scale).astype(np.float32).astype(dtype).astype(np.float64)
    return np.moveaxis((codes * scale).reshape(v.shape), -1, axis)


WIDE = False


def mx_kscale(k):
    if not WIDE:
        return np.ones(k)
    levels = np.array([30, -30])
    if k % 512:
        return np.exp2(np.random.permutation(np.resize(levels, k // 32))).repeat(32)
    a = np.empty((k // 512, 16))
    for p in range(k // 512):
        a[p, :8] = np.random.permutation(np.resize(levels, 8))
        for g in range(8):
            far = levels[np.abs(levels - a[p, g]) >= 10]
            a[p, g + 8] = far[np.random.randint(len(far))]
    return np.exp2(a.ravel()).repeat(32)


def f64(x):
    return np.asarray(x).astype(np.float64)


def striped(idx):
    return np.tile(np.asarray(idx).reshape(-1, 16).T, (8, 1)).astype(np.uint16)


def unstriped(offs):
    return offs[:16].T.reshape(-1).astype(np.int64)


def striped8(idx):
    return np.asarray(idx).reshape(8, -1, 16).transpose(0, 2, 1).reshape(128, -1).astype(np.uint16)


def unstriped8(offs):
    return offs.reshape(8, 16, -1).transpose(0, 2, 1).reshape(8, -1).astype(np.int64)


def pick8(x, idx, run):
    r = np.arange(len(x))
    return x[r[:, None], idx[r % (8 * run) // run]]


E2M1 = np.array([0.0, 0.5, 1.0, 1.5, 2.0, 3.0, 4.0, 6.0, -0.0, -0.5, -1.0, -1.5, -2.0, -3.0, -4.0, -6.0])


def pack_weight(w, fmt):
    k, n = w.shape
    w = f64(np.asarray(w, np.float32).astype(ml_dtypes.bfloat16)).reshape(k // 32, 32, n)
    amax = np.abs(w).max(1)
    if fmt in ("e4m3", "e5m2"):
        byte = np.frexp(amax)[1] - 1 + 127 - (7 if fmt == "e4m3" else 14)
    else:
        mant, ex = np.frexp(amax / 6.0)
        byte = np.where(mant > 0.5, ex, ex - 1) + 127
    byte = np.clip(np.where(amax > 0, byte, 1), 1, 254)
    scaled = (w * np.exp2(127.0 - byte)[:, None, :]).reshape(k, n).astype(np.float32)
    by_word = np.ascontiguousarray(scaled.reshape(k // 512, 128, 4, n).transpose(0, 1, 3, 2))
    if fmt in ("e4m3", "e5m2"):
        words = by_word.astype(ml_dtypes.float8_e4m3fn if fmt == "e4m3" else ml_dtypes.float8_e5m2).view(np.uint8)
    else:
        c = by_word.astype(ml_dtypes.float4_e2m1fn).view(np.uint8) & 0xF
        words = (c[..., 0::2] | (c[..., 1::2] << 4)).reshape(k // 512, 128, 2 * n)
    return np.ascontiguousarray(words), np.ascontiguousarray(byte.astype(np.uint8).reshape(k // 512, 16, n))


def unpack_weight(words, scales, fmt):
    g, _, n = scales.shape
    words = np.ascontiguousarray(words).reshape(g, 128, n, -1)
    if fmt in ("e4m3", "e5m2"):
        vals = words.view(ml_dtypes.float8_e4m3fn if fmt == "e4m3" else ml_dtypes.float8_e5m2).astype(np.float64)
    else:
        nib = np.empty((g, 128, n, 4), np.uint8)
        nib[..., 0::2] = words & 0xF
        nib[..., 1::2] = words >> 4
        vals = E2M1[nib]
    vals = vals * np.repeat(np.exp2(scales.astype(np.float64) - 127.0), 8, axis=1)[..., None]
    return vals.transpose(0, 1, 3, 2).reshape(g * 512, n)


def sgn(shape):
    return np.random.uniform(0.5, 2.0, shape) * np.where(np.random.standard_normal(shape) < 0, -1.0, 1.0)


K, T, J, R, F, Z, C, I, O, N, E = 512, 1024, 256, 512, 512, 1024, 512, 256, 128, 256, 512


def setup_inputs():
    n = np.random.standard_normal
    idx = np.random.permutation(T)[:J]
    idx2 = np.random.permutation(Z)[:J]
    idx3 = np.stack([np.random.permutation(C)[:J] for _ in range(8)])
    idx4 = np.stack([np.random.permutation(C)[:I] for _ in range(8)])
    idx5 = np.random.permutation(T)[:O]
    idx6 = np.random.permutation(E)[:O]
    idx7 = np.random.permutation(E)[:O]
    fk = mx_kscale(K)
    ff = mx_kscale(F)
    fr = mx_kscale(R)
    xtp = pack_weight(n((K, T)) / fk[:, None], "e5m2")
    xop = pack_weight(n((F, Z)) / ff[:, None], "e4m3")
    wp = pack_weight(n((K, R)) * 1 / np.sqrt(K) * fk[:, None] * fr, "e2m1")
    w0p = pack_weight(n((F, R)) * 1 / np.sqrt(F) * ff[:, None] * fr, "e2m1")
    wbp = pack_weight(n((R, N)) * 1 / np.sqrt(R) / fr[:, None], "e2m1")
    wsp = pack_weight(n((K, N)) * 1 / np.sqrt(K) * fk[:, None], "e2m1")
    return {
        "xt_words": xtp[0],
        "xt_scales": xtp[1],
        "xo_words": xop[0],
        "xo_scales": xop[1],
        "w_words": wp[0],
        "w_scales": wp[1],
        "w0_words": w0p[0],
        "w0_scales": w0p[1],
        "sa": (sgn((R, 1))).astype(np.float32),
        "wb_words": wbp[0],
        "wb_scales": wbp[1],
        "ws_words": wsp[0],
        "ws_scales": wsp[1],
        "offs": striped(idx),
        "offs2": striped(idx2),
        "offs3": striped8(idx3),
        "offs4": striped8(idx4),
        "offs5": striped(idx5),
        "offs6": striped(idx6),
        "offs7": striped(idx7),
    }


def reference(xt_words, xt_scales, xo_words, xo_scales, w_words, w_scales, w0_words, w0_scales, sa, wb_words, wb_scales, ws_words, ws_scales, offs, offs2, offs3, offs4, offs5, offs6, offs7):
    idx = unstriped(offs)
    idx2 = unstriped(offs2)
    idx3 = unstriped8(offs3)
    idx4 = unstriped8(offs4)
    idx5 = unstriped(offs5)
    idx6 = unstriped(offs6)
    idx7 = unstriped(offs7)
    xtu = unpack_weight(xt_words, xt_scales, "e5m2")
    xou = unpack_weight(xo_words, xo_scales, "e4m3")
    wu = unpack_weight(w_words, w_scales, "e2m1")
    w0u = unpack_weight(w0_words, w0_scales, "e2m1")
    wbu = unpack_weight(wb_words, wb_scales, "e2m1")
    wsu = unpack_weight(ws_words, ws_scales, "e2m1")
    xtidxg = xtu[:, idx]
    xoidx2g = xou[:, idx2]
    a = wu.T @ xtidxg + w0u.T @ xoidx2g
    pw = np.zeros((R, C))
    pw[np.arange(R)[:, None], idx3[np.arange(R) % 512 // 64]] = a
    h1 = pick8(pw, idx4, 64) * f64(sa)
    hid = h1.reshape(R, O, I // O).max(axis=2)
    hidq = mxq(hid, 0, "e4m3")
    xtidx5g = xtu[:, idx5]
    p = wbu.T @ hidq + wsu.T @ xtidx5g
    pa = np.zeros((N, E))
    pa[:, idx6] = p
    pb = np.zeros((N, E))
    pb[:, idx7] = p
    y = pa + pb
    return y

@@ -1,0 +1,215 @@
+from contextlib import ExitStack
+
+import concourse.mybir as mybir
+
+K, T, J, R, C, I, O, N, E = 512, 1024, 256, 512, 512, 256, 128, 256, 512
+FLOPS = 2 * (2 * K * R * J + 2 * R * N * O)
+
+F32 = mybir.dt.float32
+BF16 = mybir.dt.bfloat16
+I32 = mybir.dt.int32
+U32 = mybir.dt.uint32
+U16 = mybir.dt.uint16
+U8 = mybir.dt.uint8
+E4M3 = mybir.dt.float8_e4m3fn_x4
+E5M2 = mybir.dt.float8_e5m2_x4
+E2M1 = mybir.dt.float4_e2m1fn_x4
+COPY = mybir.ActivationFunctionType.Copy
+ALU = mybir.AluOpType
+
+P = 128
+PACK = 4
+QUADS = 4
+HALF = J // 2
+
+
+def tile_list_ownpool_bank_further_pagetwice_kernel(
+    tc, xt_words, xt_scales, xo_words, xo_scales, w_words, w_scales, w0_words, w0_scales, sa,
+    wb_words, wb_scales, ws_words, ws_scales, offs, offs2, offs3, offs4, offs5, offs6, offs7, out,
+):
+    nc = tc.nc
+    with ExitStack() as ctx:
+        lists = ctx.enter_context(tc.tile_pool(name="lists", bufs=1))
+        sb = ctx.enter_context(tc.tile_pool(name="sb", bufs=1))
+        psum = ctx.enter_context(tc.psum_pool(name="psum", bufs=1))
+
+        def tile(name, shape, dtype, tag=None):
+            return sb.tile(shape, dtype, name=name, tag=tag or name, align_bytes=64)
+
+        def load_list(name, src):
+            dst = lists.tile(list(src.shape), U16, name=name)
+            nc.sync.dma_start(dst[:], src)
+            return dst
+
+        def quad_rows(plane, q):
+            return plane[32 * q : 32 * q + 4, :].bitcast(I32)
+
+        def load_plane_rows(plane, scales, q):
+            nc.sync.dma_start(quad_rows(plane, q), scales[0, 4 * q : 4 * q + 4, :].bitcast(I32))
+
+        def load_staged(name, scales):
+            staged = tile(name, [4, QUADS, R // 4], I32)
+            nc.sync.dma_start(staged[:], scales[0].bitcast(I32).rearrange("(q r) c -> r q c", r=4))
+            return staged
+
+        xt_plane = tile("xt_plane", [P, T], U8)
+        xo_plane = tile("xo_plane", [P, T], U8)
+        w_plane = tile("w_plane", [P, R], U8)
+        w0_plane = tile("w0_plane", [P, R], U8)
+        wb_plane = tile("wb_plane", [P, N], U8)
+        ws_plane = tile("ws_plane", [P, N], U8)
+        boards = [tile("board%d" % b, [P, C], F32) for b in range(2)]
+        for plane in (xt_plane, xo_plane, w_plane, w0_plane):
+            nc.vector.memset(plane[:].bitcast(I32), 0)
+        for board in boards:
+            nc.vector.memset(board[:], 0.0)
+        for plane in (wb_plane, ws_plane):
+            nc.vector.memset(plane[:].bitcast(I32), 0)
+
+        w_raw = tile("w_raw", [P, 2 * R], U8)
+        w0_raw = tile("w0_raw", [P, 2 * R], U8)
+        xt_tab = tile("xt_tab", [P, T], U32)
+        xo_tab = tile("xo_tab", [P, T], U32)
+        w_staged = load_staged("w_staged", w_scales)
+        w0_staged = load_staged("w0_staged", w0_scales)
+        nc.scalar.dma_start(w_raw[:].bitcast(I32), w_words[0].bitcast(I32))
+        nc.scalar.dma_start(w0_raw[:].bitcast(I32), w0_words[0].bitcast(I32))
+        nc.scalar.dma_start(xt_tab[:].bitcast(I32), xt_words[0].rearrange("p c r -> p (c r)").bitcast(I32))
+        l1 = load_list("l1", offs)
+        for q in range(QUADS):
+            load_plane_rows(xt_plane, xt_scales, q)
+        l2 = load_list("l2", offs2)
+        load_plane_rows(xo_plane, xo_scales, 0)
+        nc.sync.dma_start(xo_tab[:].bitcast(I32), xo_words[0].rearrange("p c r -> p (c r)").bitcast(I32))
+        for q in range(1, QUADS):
+            load_plane_rows(xo_plane, xo_scales, q)
+        l3 = load_list("l3", offs3)
+        l4 = load_list("l4", offs4)
+        sa_t = tile("sa_t", [P, PACK], F32)
+        nc.sync.dma_start(sa_t[:], sa.rearrange("(p t) o -> p (t o)", t=PACK))
+        l5 = load_list("l5", offs5)
+        ws_tab = tile("ws_tab", [P, 2 * N], U8)
+        wb_tab = tile("wb_tab", [P, 2 * N], U8)
+        nc.sync.dma_start(ws_tab[:].bitcast(I32), ws_words[0].bitcast(I32))
+        for q in range(QUADS):
+            load_plane_rows(ws_plane, ws_scales, q)
+        nc.sync.dma_start(wb_tab[:].bitcast(I32), wb_words[0].bitcast(I32))
+        for q in range(QUADS):
+            load_plane_rows(wb_plane, wb_scales, q)
+        l6 = load_list("l6", offs6)
+        l7 = load_list("l7", offs7)
+
+        w_dealt = tile("w_dealt", [P, 2 * R], U8)
+        w0_dealt = tile("w0_dealt", [P, 2 * R], U8)
+        for raw, dealt in ((w_raw, w_dealt), (w0_raw, w0_dealt)):
+            nc.scalar.copy(
+                dealt[:].bitcast(U16).rearrange("p (t m) -> p t m", t=PACK),
+                raw[:].bitcast(U16).rearrange("p (m t) -> p t m", t=PACK),
+            )
+        for q in range(QUADS):
+            for staged, plane in ((w_staged, w_plane), (w0_staged, w0_plane)):
+                nc.vector.tensor_copy(quad_rows(plane, q), staged[:, q, :])
+        w_sc = tile("w_sc", [P, R], U8)
+        w0_sc = tile("w0_sc", [P, R], U8)
+
+        def deal_scales(t0, t1):
+            for plane, dealt in ((w_plane, w_sc), (w0_plane, w0_sc)):
+                nc.vector.tensor_copy(
+                    dealt[:].rearrange("p (t m) -> p t m", t=PACK)[:, t0:t1, :],
+                    plane[:].rearrange("p (m t) -> p t m", t=PACK)[:, t0:t1, :],
+                )
+
+        xt_g = tile("xt_g", [P, J], U32)
+        xt_gs = tile("xt_gs", [P, J], U8)
+        xo_g = tile("xo_g", [P, J], U32)
+        xo_gs = tile("xo_gs", [P, J], U8)
+
+        def gather_half(h):
+            cols = slice(h * HALF, (h + 1) * HALF)
+            ent = slice(h * HALF // 16, (h + 1) * HALF // 16)
+            nc.vector.tensor_copy(xt_gs[:, cols], xt_plane[:].indirect(l1[:, ent]))
+            nc.vector.tensor_copy(xt_g[:, cols], xt_tab[:].indirect(l1[:, ent]))
+            nc.vector.tensor_copy(xo_gs[:, cols], xo_plane[:].indirect(l2[:, ent]))
+            nc.vector.tensor_copy(xo_g[:, cols], xo_tab[:].indirect(l2[:, ent]))
+
+        def hidden(t, j0, j1):
+            bank = psum.tile([P, j1 - j0], F32, name="a_bank%d_%d" % (t, j0))
+            nc.tensor.matmul_mx(
+                bank[:], lhsT=w_dealt[:, 256 * t : 256 * (t + 1)].bitcast(E2M1), lhsT_scale=w_sc[:, P * t : P * (t + 1)],
+                rhs=xt_g[:, j0:j1].bitcast(E5M2), rhs_scale=xt_gs[:, j0:j1], start=True, stop=False,
+            )
+            nc.tensor.matmul_mx(
+                bank[:], lhsT=w0_dealt[:, 256 * t : 256 * (t + 1)].bitcast(E2M1), lhsT_scale=w0_sc[:, P * t : P * (t + 1)],
+                rhs=xo_g[:, j0:j1].bitcast(E4M3), rhs_scale=xo_gs[:, j0:j1], start=False, stop=True,
+            )
+            return bank
+
+        a_sb = [tile("a_sb%d" % t, [P, J], F32) for t in range(PACK)]
+        picks = [tile("picks%d" % t, [P, I], F32) for t in range(PACK)]
+        hid = tile("hid", [P, O, PACK], BF16)
+
+        def put(t, j0, j1):
+            nc.scalar.activation(boards[t % 2][:].indirect(l3[:, j0 // 16 : j1 // 16]), a_sb[t][:, j0:j1], COPY)
+
+        def pick(t):
+            nc.scalar.activation(picks[t][:], boards[t % 2][:].indirect(l4[:]), COPY, scale=sa_t[:, t : t + 1])
+            pairs = picks[t][:].rearrange("p (o two) -> p o two", two=2)
+            nc.vector.tensor_tensor(hid[:, :, t], pairs[:, :, 0], pairs[:, :, 1], ALU.max)
+
+        deal_scales(0, 1)
+        gather_half(0)
+        bank = hidden(0, 0, HALF)
+        nc.scalar.copy(a_sb[0][:, 0:HALF], bank[:])
+        put(0, 0, HALF)
+        deal_scales(1, PACK)
+        bank = hidden(1, 0, HALF)
+        nc.vector.tensor_copy(a_sb[1][:, 0:HALF], bank[:])
+        put(1, 0, HALF)
+        gather_half(1)
+        for t in range(2):
+            bank = hidden(t, HALF, J)
+            nc.vector.tensor_copy(a_sb[t][:, HALF:J], bank[:])
+            put(t, HALF, J)
+        for t in range(2, PACK):
+            bank = hidden(t, 0, J)
+            nc.vector.tensor_copy(a_sb[t][:], bank[:])
+
+        xs_g = tile("xs_g", [P, O], U32)
+        xs_gs = tile("xs_gs", [P, O], U8)
+        nc.vector.tensor_copy(xs_gs[:], xt_plane[:].indirect(l5[:]))
+        nc.vector.tensor_copy(xs_g[:], xt_tab[:].indirect(l5[:]))
+        p_banks = [psum.tile([P, O], F32, name="p_bank%d" % u) for u in range(2)]
+        for u in range(2):
+            nc.tensor.matmul_mx(
+                p_banks[u][:], lhsT=ws_tab[:, 256 * u : 256 * (u + 1)].bitcast(E2M1), lhsT_scale=ws_plane[:, P * u : P * (u + 1)],
+                rhs=xs_g[:].bitcast(E5M2), rhs_scale=xs_gs[:], start=True, stop=False,
+            )
+        page_a = [tile("page_a%d" % u, [P, E], F32, tag=("xo_tab", "xo_plane")[u]) for u in range(2)]
+        page_b = [tile("page_b%d" % u, [P, E], F32, tag=("xt_tab", "xt_plane")[u]) for u in range(2)]
+        for page in page_a + page_b:
+            nc.vector.memset(page[:], 0.0)
+
+        for t in range(2):
+            pick(t)
+        for t in range(2, PACK):
+            put(t, 0, J)
+        for t in range(2, PACK):
+            pick(t)
+
+        hid_q = tile("hid_q", [P, O], U32)
+        hid_s = tile("hid_s", [P, O], U8)
+        nc.vector.quantize_mx(hid_q[:].bitcast(E4M3), hid_s[:], hid[:].rearrange("p o t -> p (o t)"))
+        for u in range(2):
+            nc.tensor.matmul_mx(
+                p_banks[u][:], lhsT=wb_tab[:, 256 * u : 256 * (u + 1)].bitcast(E2M1), lhsT_scale=wb_plane[:, P * u : P * (u + 1)],
+                rhs=hid_q[:].bitcast(E4M3), rhs_scale=hid_s[:], start=False, stop=True,
+            )
+        p_sb = [tile("p_sb%d" % u, [P, O], F32) for u in range(2)]
+        nc.vector.tensor_copy(p_sb[0][:], p_banks[0][:])
+        nc.scalar.copy(p_sb[1][:], p_banks[1][:])
+        for u in range(2):
+            y = tile("y%d" % u, [P, E], F32)
+            nc.scalar.activation(page_b[u][:].indirect(l7[:]), p_sb[u][:], COPY)
+            nc.vector.tensor_copy(page_a[u][:].indirect(l6[:]), p_sb[u][:])
+            nc.vector.tensor_tensor(y[:], page_a[u][:], page_b[u][:], ALU.add)
+            nc.sync.dma_start(out[P * u : P * (u + 1), :], y[:])

@@ -44,11 +44,11 @@ def tile_list_ownpool_bank_further_pagetwice_kernel(
         def quad_rows(plane, q):
             return plane[32 * q : 32 * q + 4, :].bitcast(I32)
 
-        def load_plane_rows(plane, scales, q):
-            nc.sync.dma_start(quad_rows(plane, q), scales[0, 4 * q : 4 * q + 4, :].bitcast(I32))
+        def load_plane_rows(plane, scales, q, queue=nc.sync):
+            queue.dma_start(quad_rows(plane, q), scales[0, 4 * q : 4 * q + 4, :].bitcast(I32))
 
         def load_staged(name, scales):
-            staged = tile(name, [4, QUADS, R // 4], I32)
+            staged = tile(name, [4, QUADS, scales.shape[2] // 4], I32)
             nc.sync.dma_start(staged[:], scales[0].bitcast(I32).rearrange("(q r) c -> r q c", r=4))
             return staged
 
@@ -58,8 +58,8 @@ def tile_list_ownpool_bank_further_pagetwice_kernel(
         w0_plane = tile("w0_plane", [P, R], U8)
         wb_plane = tile("wb_plane", [P, N], U8)
         ws_plane = tile("ws_plane", [P, N], U8)
-        boards = [tile("board%d" % b, [P, C], F32) for b in range(2)]
-        for plane in (xt_plane, xo_plane, w_plane, w0_plane):
+        boards = [tile("board%d" % b, [P, C], F32) for b in range(PACK)]
+        for plane in (xo_plane, w_plane, w0_plane, xt_plane):
             nc.vector.memset(plane[:].bitcast(I32), 0)
         for board in boards:
             nc.vector.memset(board[:], 0.0)
@@ -72,17 +72,14 @@ def tile_list_ownpool_bank_further_pagetwice_kernel(
         xo_tab = tile("xo_tab", [P, T], U32)
         w_staged = load_staged("w_staged", w_scales)
         w0_staged = load_staged("w0_staged", w0_scales)
-        nc.scalar.dma_start(w_raw[:].bitcast(I32), w_words[0].bitcast(I32))
-        nc.scalar.dma_start(w0_raw[:].bitcast(I32), w0_words[0].bitcast(I32))
-        nc.scalar.dma_start(xt_tab[:].bitcast(I32), xt_words[0].rearrange("p c r -> p (c r)").bitcast(I32))
-        l1 = load_list("l1", offs)
-        for q in range(QUADS):
-            load_plane_rows(xt_plane, xt_scales, q)
-        l2 = load_list("l2", offs2)
-        load_plane_rows(xo_plane, xo_scales, 0)
+        xt_staged = load_staged("xt_staged", xt_scales)
+        xo_staged = load_staged("xo_staged", xo_scales)
+        nc.sync.dma_start(w_raw[:].bitcast(I32), w_words[0].bitcast(I32))
+        nc.sync.dma_start(w0_raw[:].bitcast(I32), w0_words[0].bitcast(I32))
+        nc.sync.dma_start(xt_tab[:].bitcast(I32), xt_words[0].rearrange("p c r -> p (c r)").bitcast(I32))
         nc.sync.dma_start(xo_tab[:].bitcast(I32), xo_words[0].rearrange("p c r -> p (c r)").bitcast(I32))
-        for q in range(1, QUADS):
-            load_plane_rows(xo_plane, xo_scales, q)
+        l1 = load_list("l1", offs)
+        l2 = load_list("l2", offs2)
         l3 = load_list("l3", offs3)
         l4 = load_list("l4", offs4)
         sa_t = tile("sa_t", [P, PACK], F32)
@@ -107,75 +104,80 @@ def tile_list_ownpool_bank_further_pagetwice_kernel(
                 raw[:].bitcast(U16).rearrange("p (m t) -> p t m", t=PACK),
             )
         for q in range(QUADS):
-            for staged, plane in ((w_staged, w_plane), (w0_staged, w0_plane)):
+            for staged, plane in ((w_staged, w_plane), (w0_staged, w0_plane), (xt_staged, xt_plane), (xo_staged, xo_plane)):
                 nc.vector.tensor_copy(quad_rows(plane, q), staged[:, q, :])
-        w_sc = tile("w_sc", [P, R], U8)
-        w0_sc = tile("w0_sc", [P, R], U8)
+        dealt_scales = {}
 
-        def deal_scales(t0, t1):
-            for plane, dealt in ((w_plane, w_sc), (w0_plane, w0_sc)):
-                nc.vector.tensor_copy(
-                    dealt[:].rearrange("p (t m) -> p t m", t=PACK)[:, t0:t1, :],
-                    plane[:].rearrange("p (m t) -> p t m", t=PACK)[:, t0:t1, :],
-                )
-
-        xt_g = tile("xt_g", [P, J], U32)
-        xt_gs = tile("xt_gs", [P, J], U8)
-        xo_g = tile("xo_g", [P, J], U32)
-        xo_gs = tile("xo_gs", [P, J], U8)
+        def deal_scales(t):
+            pair = []
+            for name, plane in (("w_sc", w_plane), ("w0_sc", w0_plane)):
+                dealt = tile("%s%d" % (name, t), [P, P], U8, tag="%s%d" % (name, t))
+                nc.vector.tensor_copy(dealt[:], plane[:].rearrange("p (m t) -> p t m", t=PACK)[:, t, :])
+                pair.append(dealt)
+            dealt_scales[t] = pair
 
         def gather_half(h):
-            cols = slice(h * HALF, (h + 1) * HALF)
             ent = slice(h * HALF // 16, (h + 1) * HALF // 16)
-            nc.vector.tensor_copy(xt_gs[:, cols], xt_plane[:].indirect(l1[:, ent]))
-            nc.vector.tensor_copy(xt_g[:, cols], xt_tab[:].indirect(l1[:, ent]))
-            nc.vector.tensor_copy(xo_gs[:, cols], xo_plane[:].indirect(l2[:, ent]))
-            nc.vector.tensor_copy(xo_g[:, cols], xo_tab[:].indirect(l2[:, ent]))
+            xt_gs = tile("xt_gs%d" % h, [P, HALF], U8, tag="xt_gs")
+            xt_g = tile("xt_g%d" % h, [P, HALF], U32, tag="xt_g")
+            xo_gs = tile("xo_gs%d" % h, [P, HALF], U8, tag="xo_gs")
+            xo_g = tile("xo_g%d" % h, [P, HALF], U32, tag="xo_g")
+            nc.vector.tensor_copy(xt_gs[:], xt_plane[:].indirect(l1[:, ent]))
+            nc.vector.tensor_copy(xt_g[:], xt_tab[:].indirect(l1[:, ent]))
+            nc.vector.tensor_copy(xo_gs[:], xo_plane[:].indirect(l2[:, ent]))
+            nc.vector.tensor_copy(xo_g[:], xo_tab[:].indirect(l2[:, ent]))
+            return xt_g, xt_gs, xo_g, xo_gs
 
-        def hidden(t, j0, j1):
-            bank = psum.tile([P, j1 - j0], F32, name="a_bank%d_%d" % (t, j0))
-            nc.tensor.matmul_mx(
-                bank[:], lhsT=w_dealt[:, 256 * t : 256 * (t + 1)].bitcast(E2M1), lhsT_scale=w_sc[:, P * t : P * (t + 1)],
-                rhs=xt_g[:, j0:j1].bitcast(E5M2), rhs_scale=xt_gs[:, j0:j1], start=True, stop=False,
-            )
-            nc.tensor.matmul_mx(
-                bank[:], lhsT=w0_dealt[:, 256 * t : 256 * (t + 1)].bitcast(E2M1), lhsT_scale=w0_sc[:, P * t : P * (t + 1)],
-                rhs=xo_g[:, j0:j1].bitcast(E4M3), rhs_scale=xo_gs[:, j0:j1], start=False, stop=True,
-            )
+        def hidden(gathered, ts, name):
+            xt_g, xt_gs, xo_g, xo_gs = gathered
+            bank = psum.tile([P, len(ts), HALF], F32, name=name)
+            for k, t in enumerate(ts):
+                nc.tensor.matmul_mx(
+                    bank[:, k, :], lhsT=w_dealt[:, 256 * t : 256 * (t + 1)].bitcast(E2M1), lhsT_scale=dealt_scales[t][0][:],
+                    rhs=xt_g[:].bitcast(E5M2), rhs_scale=xt_gs[:], start=True, stop=False,
+                )
+                nc.tensor.matmul_mx(
+                    bank[:, k, :], lhsT=w0_dealt[:, 256 * t : 256 * (t + 1)].bitcast(E2M1), lhsT_scale=dealt_scales[t][1][:],
+                    rhs=xo_g[:].bitcast(E4M3), rhs_scale=xo_gs[:], start=False, stop=True,
+                )
             return bank
 
-        a_sb = [tile("a_sb%d" % t, [P, J], F32) for t in range(PACK)]
         picks = [tile("picks%d" % t, [P, I], F32) for t in range(PACK)]
         hid = tile("hid", [P, O, PACK], BF16)
 
-        def put(t, j0, j1):
-            nc.scalar.activation(boards[t % 2][:].indirect(l3[:, j0 // 16 : j1 // 16]), a_sb[t][:, j0:j1], COPY)
+        def put(t, h, values):
+            nc.scalar.activation(boards[t][:].indirect(l3[:, h * HALF // 16 : (h + 1) * HALF // 16]), values, COPY)
 
         def pick(t):
-            nc.scalar.activation(picks[t][:], boards[t % 2][:].indirect(l4[:]), COPY, scale=sa_t[:, t : t + 1])
+            nc.scalar.activation(picks[t][:], boards[t][:].indirect(l4[:]), COPY, scale=sa_t[:, t : t + 1])
             pairs = picks[t][:].rearrange("p (o two) -> p o two", two=2)
             nc.vector.tensor_tensor(hid[:, :, t], pairs[:, :, 0], pairs[:, :, 1], ALU.max)
 
-        deal_scales(0, 1)
-        gather_half(0)
-        bank = hidden(0, 0, HALF)
-        nc.scalar.copy(a_sb[0][:, 0:HALF], bank[:])
-        put(0, 0, HALF)
-        deal_scales(1, PACK)
-        bank = hidden(1, 0, HALF)
-        nc.vector.tensor_copy(a_sb[1][:, 0:HALF], bank[:])
-        put(1, 0, HALF)
-        gather_half(1)
-        for t in range(2):
-            bank = hidden(t, HALF, J)
-            nc.vector.tensor_copy(a_sb[t][:, HALF:J], bank[:])
-            put(t, HALF, J)
-        for t in range(2, PACK):
-            bank = hidden(t, 0, J)
-            nc.vector.tensor_copy(a_sb[t][:], bank[:])
+        def make_hidden(gathered, h, ts, copy):
+            name = "a%d_%d" % (h, ts[0])
+            bank = hidden(gathered, ts, name + "_bank")
+            values = tile(name, [P, len(ts), HALF], F32)
+            copy(values[:], bank[:])
+            return values
 
-        xs_g = tile("xs_g", [P, O], U32)
-        xs_gs = tile("xs_gs", [P, O], U8)
+        deal_scales(0)
+        gathered = gather_half(0)
+        a00 = make_hidden(gathered, 0, [0], nc.scalar.copy)
+        put(0, 0, a00[:, 0, :])
+        deal_scales(1)
+        a01 = make_hidden(gathered, 0, [1], nc.vector.tensor_copy)
+        put(1, 0, a01[:, 0, :])
+        deal_scales(2)
+        deal_scales(3)
+        a02 = make_hidden(gathered, 0, [2, 3], nc.vector.tensor_copy)
+        put(2, 0, a02[:, 0, :])
+        put(3, 0, a02[:, 1, :])
+        gathered = gather_half(1)
+        a10 = make_hidden(gathered, 1, [0, 1], nc.vector.tensor_copy)
+        a12 = make_hidden(gathered, 1, [2, 3], nc.vector.tensor_copy)
+
+        xs_g = tile("xs_g", [P, O], U32, tag="xo_g")
+        xs_gs = tile("xs_gs", [P, O], U8, tag="xo_gs")
         nc.vector.tensor_copy(xs_gs[:], xt_plane[:].indirect(l5[:]))
         nc.vector.tensor_copy(xs_g[:], xt_tab[:].indirect(l5[:]))
         p_banks = [psum.tile([P, O], F32, name="p_bank%d" % u) for u in range(2)]
@@ -189,12 +191,14 @@ def tile_list_ownpool_bank_further_pagetwice_kernel(
         for page in page_a + page_b:
             nc.vector.memset(page[:], 0.0)
 
-        for t in range(2):
-            pick(t)
-        for t in range(2, PACK):
-            put(t, 0, J)
-        for t in range(2, PACK):
-            pick(t)
+        put(0, 1, a10[:, 0, :])
+        put(1, 1, a10[:, 1, :])
+        pick(0)
+        put(2, 1, a12[:, 0, :])
+        pick(1)
+        put(3, 1, a12[:, 1, :])
+        pick(2)
+        pick(3)
 
         hid_q = tile("hid_q", [P, O], U32)
         hid_s = tile("hid_s", [P, O], U8)
@@ -211,5 +215,8 @@ def tile_list_ownpool_bank_further_pagetwice_kernel(
             y = tile("y%d" % u, [P, E], F32)
             nc.scalar.activation(page_b[u][:].indirect(l7[:]), p_sb[u][:], COPY)
             nc.vector.tensor_copy(page_a[u][:].indirect(l6[:]), p_sb[u][:])
-            nc.vector.tensor_tensor(y[:], page_a[u][:], page_b[u][:], ALU.add)
-            nc.sync.dma_start(out[P * u : P * (u + 1), :], y[:])
+            pieces = 1 + u
+            for k in range(pieces):
+                cols = slice(k * E // pieces, (k + 1) * E // pieces)
+                nc.vector.tensor_tensor(y[:, cols], page_a[u][:, cols], page_b[u][:, cols], ALU.add)
+                (nc.sync, nc.scalar)[k].dma_start(out[P * u : P * (u + 1), cols], y[:, cols])

@@ -47,39 +47,39 @@ def tile_list_ownpool_bank_further_pagetwice_kernel(
         def load_plane_rows(plane, scales, q, queue=nc.sync):
             queue.dma_start(quad_rows(plane, q), scales[0, 4 * q : 4 * q + 4, :].bitcast(I32))
 
-        def load_staged(name, scales):
-            staged = tile(name, [4, QUADS, scales.shape[2] // 4], I32)
-            nc.sync.dma_start(staged[:], scales[0].bitcast(I32).rearrange("(q r) c -> r q c", r=4))
-            return staged
-
         xt_plane = tile("xt_plane", [P, T], U8)
         xo_plane = tile("xo_plane", [P, T], U8)
-        w_plane = tile("w_plane", [P, R], U8)
-        w0_plane = tile("w0_plane", [P, R], U8)
+        w_planes = tile("w_planes", [P, 2 * R], U8)
         wb_plane = tile("wb_plane", [P, N], U8)
         ws_plane = tile("ws_plane", [P, N], U8)
         boards = [tile("board%d" % b, [P, C], F32) for b in range(PACK)]
-        for plane in (xo_plane, w_plane, w0_plane, xt_plane):
+        for plane in (xt_plane, xo_plane, w_planes):
             nc.vector.memset(plane[:].bitcast(I32), 0)
         for board in boards:
             nc.vector.memset(board[:], 0.0)
-        for plane in (wb_plane, ws_plane):
+        hid_q = tile("hid_q", [P, O], U32)
+        hid_s = tile("hid_s", [P, O], U8)
+        for plane in (wb_plane, ws_plane, hid_s):
             nc.vector.memset(plane[:].bitcast(I32), 0)
+        nc.vector.memset(hid_q[:, O // 2 :].bitcast(I32), 0)
 
         w_raw = tile("w_raw", [P, 2 * R], U8)
         w0_raw = tile("w0_raw", [P, 2 * R], U8)
         xt_tab = tile("xt_tab", [P, T], U32)
         xo_tab = tile("xo_tab", [P, T], U32)
-        w_staged = load_staged("w_staged", w_scales)
-        w0_staged = load_staged("w0_staged", w0_scales)
-        xt_staged = load_staged("xt_staged", xt_scales)
-        xo_staged = load_staged("xo_staged", xo_scales)
-        nc.sync.dma_start(w_raw[:].bitcast(I32), w_words[0].bitcast(I32))
-        nc.sync.dma_start(w0_raw[:].bitcast(I32), w0_words[0].bitcast(I32))
-        nc.sync.dma_start(xt_tab[:].bitcast(I32), xt_words[0].rearrange("p c r -> p (c r)").bitcast(I32))
-        nc.sync.dma_start(xo_tab[:].bitcast(I32), xo_words[0].rearrange("p c r -> p (c r)").bitcast(I32))
+        w_staged = tile("w_staged", [4, QUADS, 2, R // 4], I32)
+        for k, scales in enumerate((w_scales, w0_scales)):
+            nc.sync.dma_start(w_staged[:, :, k, :], scales[0].bitcast(I32).rearrange("(q r) c -> r q c", r=4))
         l1 = load_list("l1", offs)
+        nc.sync.dma_start(w_raw[:].bitcast(I32), w_words[0].bitcast(I32))
+        nc.sync.dma_start(xt_tab[:].bitcast(I32), xt_words[0].rearrange("p c r -> p (c r)").bitcast(I32))
+        for q in range(QUADS):
+            load_plane_rows(xt_plane, xt_scales, q)
+        nc.sync.dma_start(w0_raw[:].bitcast(I32), w0_words[0].bitcast(I32))
+        nc.sync.dma_start(xo_tab[:].bitcast(I32), xo_words[0].rearrange("p c r -> p (c r)").bitcast(I32))
         l2 = load_list("l2", offs2)
+        for q in range(QUADS):
+            load_plane_rows(xo_plane, xo_scales, q)
         l3 = load_list("l3", offs3)
         l4 = load_list("l4", offs4)
         sa_t = tile("sa_t", [P, PACK], F32)
@@ -104,17 +104,13 @@ def tile_list_ownpool_bank_further_pagetwice_kernel(
                 raw[:].bitcast(U16).rearrange("p (m t) -> p t m", t=PACK),
             )
         for q in range(QUADS):
-            for staged, plane in ((w_staged, w_plane), (w0_staged, w0_plane), (xt_staged, xt_plane), (xo_staged, xo_plane)):
-                nc.vector.tensor_copy(quad_rows(plane, q), staged[:, q, :])
+            nc.vector.tensor_copy(quad_rows(w_planes, q), w_staged[:, q, :, :].rearrange("r k c -> r (k c)"))
         dealt_scales = {}
 
         def deal_scales(t):
-            pair = []
-            for name, plane in (("w_sc", w_plane), ("w0_sc", w0_plane)):
-                dealt = tile("%s%d" % (name, t), [P, P], U8, tag="%s%d" % (name, t))
-                nc.vector.tensor_copy(dealt[:], plane[:].rearrange("p (m t) -> p t m", t=PACK)[:, t, :])
-                pair.append(dealt)
-            dealt_scales[t] = pair
+            dealt = tile("w_sc%d" % t, [P, 2 * P], U8)
+            nc.vector.tensor_copy(dealt[:], w_planes[:].rearrange("p (m t) -> p t m", t=PACK)[:, t, :])
+            dealt_scales[t] = dealt
 
         def gather_half(h):
             ent = slice(h * HALF // 16, (h + 1) * HALF // 16)
@@ -133,23 +129,21 @@ def tile_list_ownpool_bank_further_pagetwice_kernel(
             bank = psum.tile([P, len(ts), HALF], F32, name=name)
             for k, t in enumerate(ts):
                 nc.tensor.matmul_mx(
-                    bank[:, k, :], lhsT=w_dealt[:, 256 * t : 256 * (t + 1)].bitcast(E2M1), lhsT_scale=dealt_scales[t][0][:],
+                    bank[:, k, :], lhsT=w_dealt[:, 256 * t : 256 * (t + 1)].bitcast(E2M1), lhsT_scale=dealt_scales[t][:, 0:P],
                     rhs=xt_g[:].bitcast(E5M2), rhs_scale=xt_gs[:], start=True, stop=False,
                 )
                 nc.tensor.matmul_mx(
-                    bank[:, k, :], lhsT=w0_dealt[:, 256 * t : 256 * (t + 1)].bitcast(E2M1), lhsT_scale=dealt_scales[t][1][:],
+                    bank[:, k, :], lhsT=w0_dealt[:, 256 * t : 256 * (t + 1)].bitcast(E2M1), lhsT_scale=dealt_scales[t][:, P : 2 * P],
                     rhs=xo_g[:].bitcast(E4M3), rhs_scale=xo_gs[:], start=False, stop=True,
                 )
             return bank
 
-        picks = [tile("picks%d" % t, [P, I], F32) for t in range(PACK)]
-        hid = tile("hid", [P, O, PACK], BF16)
-
         def put(t, h, values):
             nc.scalar.activation(boards[t][:].indirect(l3[:, h * HALF // 16 : (h + 1) * HALF // 16]), values, COPY)
 
-        def pick(t):
-            nc.scalar.activation(picks[t][:], boards[t][:].indirect(l4[:]), COPY, scale=sa_t[:, t : t + 1])
+        def pick(t, h, picks, hid):
+            ent = slice(h * HALF // 16, (h + 1) * HALF // 16)
+            nc.scalar.activation(picks[t][:], boards[t][:].indirect(l4[:, ent]), COPY, scale=sa_t[:, t : t + 1])
             pairs = picks[t][:].rearrange("p (o two) -> p o two", two=2)
             nc.vector.tensor_tensor(hid[:, :, t], pairs[:, :, 0], pairs[:, :, 1], ALU.max)
 
@@ -173,48 +167,71 @@ def tile_list_ownpool_bank_further_pagetwice_kernel(
         put(2, 0, a02[:, 0, :])
         put(3, 0, a02[:, 1, :])
         gathered = gather_half(1)
-        a10 = make_hidden(gathered, 1, [0, 1], nc.vector.tensor_copy)
+        a10 = make_hidden(gathered, 1, [0], nc.vector.tensor_copy)
+        a11 = make_hidden(gathered, 1, [1], nc.vector.tensor_copy)
         a12 = make_hidden(gathered, 1, [2, 3], nc.vector.tensor_copy)
 
         xs_g = tile("xs_g", [P, O], U32, tag="xo_g")
         xs_gs = tile("xs_gs", [P, O], U8, tag="xo_gs")
         nc.vector.tensor_copy(xs_gs[:], xt_plane[:].indirect(l5[:]))
         nc.vector.tensor_copy(xs_g[:], xt_tab[:].indirect(l5[:]))
-        p_banks = [psum.tile([P, O], F32, name="p_bank%d" % u) for u in range(2)]
+        x_bank = psum.tile([P, 2, O], F32, name="x_bank")
+        y_bank = psum.tile([P, 2, O], F32, name="y_bank")
         for u in range(2):
             nc.tensor.matmul_mx(
-                p_banks[u][:], lhsT=ws_tab[:, 256 * u : 256 * (u + 1)].bitcast(E2M1), lhsT_scale=ws_plane[:, P * u : P * (u + 1)],
-                rhs=xs_g[:].bitcast(E5M2), rhs_scale=xs_gs[:], start=True, stop=False,
+                x_bank[:, u, :], lhsT=ws_tab[:, 256 * u : 256 * (u + 1)].bitcast(E2M1), lhsT_scale=ws_plane[:, P * u : P * (u + 1)],
+                rhs=xs_g[:].bitcast(E5M2), rhs_scale=xs_gs[:], start=(u == 0), stop=False,
             )
         page_a = [tile("page_a%d" % u, [P, E], F32, tag=("xo_tab", "xo_plane")[u]) for u in range(2)]
         page_b = [tile("page_b%d" % u, [P, E], F32, tag=("xt_tab", "xt_plane")[u]) for u in range(2)]
         for page in page_a + page_b:
             nc.vector.memset(page[:], 0.0)
 
+        picks0 = [tile("picks0_%d" % t, [P, HALF], F32) for t in range(PACK)]
+        hid0 = tile("hid0", [P, O // 2, PACK], BF16)
         put(0, 1, a10[:, 0, :])
-        put(1, 1, a10[:, 1, :])
-        pick(0)
+        put(1, 1, a11[:, 0, :])
+        pick(0, 0, picks0, hid0)
         put(2, 1, a12[:, 0, :])
-        pick(1)
+        pick(1, 0, picks0, hid0)
         put(3, 1, a12[:, 1, :])
-        pick(2)
-        pick(3)
+        pick(2, 0, picks0, hid0)
+        pick(3, 0, picks0, hid0)
 
-        hid_q = tile("hid_q", [P, O], U32)
-        hid_s = tile("hid_s", [P, O], U8)
-        nc.vector.quantize_mx(hid_q[:].bitcast(E4M3), hid_s[:], hid[:].rearrange("p o t -> p (o t)"))
+        def pool_product(h, hid, bank, start):
+            cols = slice(h * O // 2, (h + 1) * O // 2)
+            nc.vector.quantize_mx(hid_q[:, cols].bitcast(E4M3), hid_s[:, cols], hid[:].rearrange("p o t -> p (o t)"))
+            for u in range(2):
+                nc.tensor.matmul_mx(
+                    bank[:, u, :], lhsT=wb_tab[:, 256 * u : 256 * (u + 1)].bitcast(E2M1), lhsT_scale=wb_plane[:, P * u : P * (u + 1)],
+                    rhs=hid_q[:].bitcast(E4M3), rhs_scale=hid_s[:], start=start, stop=start or u == 1,
+                )
+
+        def place(engine, page, offsets, h, values):
+            window = page[:].indirect(offsets[:, h * O // 32 : (h + 1) * O // 32])
+            if engine == "scalar":
+                nc.scalar.activation(window, values, COPY)
+            else:
+                nc.vector.tensor_copy(window, values)
+
+        pool_product(0, hid0, x_bank, False)
+        hid1 = tile("hid1", [P, O // 2, PACK], BF16, tag="hid0")
+        picks1 = [tile("picks1_%d" % t, [P, HALF], F32, tag=("a1_2", "picks0_2", None, None)[t]) for t in range(PACK)]
+        for t in (2, 3, 0, 1):
+            pick(t, 1, picks1, hid1)
+        x_sb = tile("x_sb", [P, 2, O], F32)
+        nc.scalar.copy(x_sb[:], x_bank[:])
+        pool_product(1, hid1, y_bank, True)
+        for pages, offsets in ((page_a, l6), (page_b, l7)):
+            for u in range(2):
+                place("scalar", pages[u], offsets, 0, x_sb[:, u, 0 : O // 2])
+        p_hi = tile("p_hi", [P, 2, O // 2], F32)
+        nc.vector.tensor_tensor(p_hi[:], y_bank[:, :, O // 2 :], x_sb[:, :, O // 2 :], ALU.add)
         for u in range(2):
-            nc.tensor.matmul_mx(
-                p_banks[u][:], lhsT=wb_tab[:, 256 * u : 256 * (u + 1)].bitcast(E2M1), lhsT_scale=wb_plane[:, P * u : P * (u + 1)],
-                rhs=hid_q[:].bitcast(E4M3), rhs_scale=hid_s[:], start=False, stop=True,
-            )
-        p_sb = [tile("p_sb%d" % u, [P, O], F32) for u in range(2)]
-        nc.vector.tensor_copy(p_sb[0][:], p_banks[0][:])
-        nc.scalar.copy(p_sb[1][:], p_banks[1][:])
+            place("vector", page_a[u], l6, 1, p_hi[:, u, :])
+            place("scalar", page_b[u], l7, 1, p_hi[:, u, :])
         for u in range(2):
             y = tile("y%d" % u, [P, E], F32)
-            nc.scalar.activation(page_b[u][:].indirect(l7[:]), p_sb[u][:], COPY)
-            nc.vector.tensor_copy(page_a[u][:].indirect(l6[:]), p_sb[u][:])
             pieces = 1 + u
             for k in range(pieces):
                 cols = slice(k * E // pieces, (k + 1) * E // pieces)

from contextlib import ExitStack

import concourse.mybir as mybir

K, T, J, R, C, I, O, N, E = 512, 1024, 256, 512, 512, 256, 128, 256, 512
FLOPS = 2 * (2 * K * R * J + 2 * R * N * O)

F32 = mybir.dt.float32
BF16 = mybir.dt.bfloat16
I32 = mybir.dt.int32
U32 = mybir.dt.uint32
U16 = mybir.dt.uint16
U8 = mybir.dt.uint8
E4M3 = mybir.dt.float8_e4m3fn_x4
E5M2 = mybir.dt.float8_e5m2_x4
E2M1 = mybir.dt.float4_e2m1fn_x4
COPY = mybir.ActivationFunctionType.Copy
ALU = mybir.AluOpType

P = 128
PACK = 4
QUADS = 4
HALF = J // 2


def tile_list_ownpool_bank_further_pagetwice_kernel(
    tc, xt_words, xt_scales, xo_words, xo_scales, w_words, w_scales, w0_words, w0_scales, sa,
    wb_words, wb_scales, ws_words, ws_scales, offs, offs2, offs3, offs4, offs5, offs6, offs7, out,
):
    nc = tc.nc
    with ExitStack() as ctx:
        lists = ctx.enter_context(tc.tile_pool(name="lists", bufs=1))
        sb = ctx.enter_context(tc.tile_pool(name="sb", bufs=1))
        psum = ctx.enter_context(tc.psum_pool(name="psum", bufs=1))

        def tile(name, shape, dtype, tag=None):
            return sb.tile(shape, dtype, name=name, tag=tag or name, align_bytes=64)

        def load_list(name, src):
            dst = lists.tile(list(src.shape), U16, name=name)
            nc.sync.dma_start(dst[:], src)
            return dst

        def quad_rows(plane, q):
            return plane[32 * q : 32 * q + 4, :].bitcast(I32)

        def load_plane_rows(plane, scales, q, queue=nc.sync):
            queue.dma_start(quad_rows(plane, q), scales[0, 4 * q : 4 * q + 4, :].bitcast(I32))

        xt_plane = tile("xt_plane", [P, T], U8)
        xo_plane = tile("xo_plane", [P, T], U8)
        w_planes = tile("w_planes", [P, 2 * R], U8)
        wb_plane = tile("wb_plane", [P, N], U8)
        ws_plane = tile("ws_plane", [P, N], U8)
        boards = [tile("board%d" % b, [P, C], F32) for b in range(PACK)]
        for plane in (xt_plane, xo_plane, w_planes):
            nc.vector.memset(plane[:].bitcast(I32), 0)
        for board in boards:
            nc.vector.memset(board[:], 0.0)
        hid_q = tile("hid_q", [P, O], U32)
        hid_s = tile("hid_s", [P, O], U8)
        for plane in (wb_plane, ws_plane, hid_s):
            nc.vector.memset(plane[:].bitcast(I32), 0)
        nc.vector.memset(hid_q[:, O // 2 :].bitcast(I32), 0)

        w_raw = tile("w_raw", [P, 2 * R], U8)
        w0_raw = tile("w0_raw", [P, 2 * R], U8)
        xt_tab = tile("xt_tab", [P, T], U32)
        xo_tab = tile("xo_tab", [P, T], U32)
        w_staged = tile("w_staged", [4, QUADS, 2, R // 4], I32)
        for k, scales in enumerate((w_scales, w0_scales)):
            nc.sync.dma_start(w_staged[:, :, k, :], scales[0].bitcast(I32).rearrange("(q r) c -> r q c", r=4))
        l1 = load_list("l1", offs)
        nc.sync.dma_start(w_raw[:].bitcast(I32), w_words[0].bitcast(I32))
        nc.sync.dma_start(xt_tab[:].bitcast(I32), xt_words[0].rearrange("p c r -> p (c r)").bitcast(I32))
        for q in range(QUADS):
            load_plane_rows(xt_plane, xt_scales, q)
        nc.sync.dma_start(w0_raw[:].bitcast(I32), w0_words[0].bitcast(I32))
        nc.sync.dma_start(xo_tab[:].bitcast(I32), xo_words[0].rearrange("p c r -> p (c r)").bitcast(I32))
        l2 = load_list("l2", offs2)
        for q in range(QUADS):
            load_plane_rows(xo_plane, xo_scales, q)
        l3 = load_list("l3", offs3)
        l4 = load_list("l4", offs4)
        sa_t = tile("sa_t", [P, PACK], F32)
        nc.sync.dma_start(sa_t[:], sa.rearrange("(p t) o -> p (t o)", t=PACK))
        l5 = load_list("l5", offs5)
        ws_tab = tile("ws_tab", [P, 2 * N], U8)
        wb_tab = tile("wb_tab", [P, 2 * N], U8)
        nc.sync.dma_start(ws_tab[:].bitcast(I32), ws_words[0].bitcast(I32))
        for q in range(QUADS):
            load_plane_rows(ws_plane, ws_scales, q)
        nc.sync.dma_start(wb_tab[:].bitcast(I32), wb_words[0].bitcast(I32))
        for q in range(QUADS):
            load_plane_rows(wb_plane, wb_scales, q)
        l6 = load_list("l6", offs6)
        l7 = load_list("l7", offs7)

        w_dealt = tile("w_dealt", [P, 2 * R], U8)
        w0_dealt = tile("w0_dealt", [P, 2 * R], U8)
        for raw, dealt in ((w_raw, w_dealt), (w0_raw, w0_dealt)):
            nc.scalar.copy(
                dealt[:].bitcast(U16).rearrange("p (t m) -> p t m", t=PACK),
                raw[:].bitcast(U16).rearrange("p (m t) -> p t m", t=PACK),
            )
        for q in range(QUADS):
            nc.vector.tensor_copy(quad_rows(w_planes, q), w_staged[:, q, :, :].rearrange("r k c -> r (k c)"))
        dealt_scales = {}

        def deal_scales(t):
            dealt = tile("w_sc%d" % t, [P, 2 * P], U8)
            nc.vector.tensor_copy(dealt[:], w_planes[:].rearrange("p (m t) -> p t m", t=PACK)[:, t, :])
            dealt_scales[t] = dealt

        def gather_half(h):
            ent = slice(h * HALF // 16, (h + 1) * HALF // 16)
            xt_gs = tile("xt_gs%d" % h, [P, HALF], U8, tag="xt_gs")
            xt_g = tile("xt_g%d" % h, [P, HALF], U32, tag="xt_g")
            xo_gs = tile("xo_gs%d" % h, [P, HALF], U8, tag="xo_gs")
            xo_g = tile("xo_g%d" % h, [P, HALF], U32, tag="xo_g")
            nc.vector.tensor_copy(xt_gs[:], xt_plane[:].indirect(l1[:, ent]))
            nc.vector.tensor_copy(xt_g[:], xt_tab[:].indirect(l1[:, ent]))
            nc.vector.tensor_copy(xo_gs[:], xo_plane[:].indirect(l2[:, ent]))
            nc.vector.tensor_copy(xo_g[:], xo_tab[:].indirect(l2[:, ent]))
            return xt_g, xt_gs, xo_g, xo_gs

        def hidden(gathered, ts, name):
            xt_g, xt_gs, xo_g, xo_gs = gathered
            bank = psum.tile([P, len(ts), HALF], F32, name=name)
            for k, t in enumerate(ts):
                nc.tensor.matmul_mx(
                    bank[:, k, :], lhsT=w_dealt[:, 256 * t : 256 * (t + 1)].bitcast(E2M1), lhsT_scale=dealt_scales[t][:, 0:P],
                    rhs=xt_g[:].bitcast(E5M2), rhs_scale=xt_gs[:], start=True, stop=False,
                )
                nc.tensor.matmul_mx(
                    bank[:, k, :], lhsT=w0_dealt[:, 256 * t : 256 * (t + 1)].bitcast(E2M1), lhsT_scale=dealt_scales[t][:, P : 2 * P],
                    rhs=xo_g[:].bitcast(E4M3), rhs_scale=xo_gs[:], start=False, stop=True,
                )
            return bank

        def put(t, h, values):
            nc.scalar.activation(boards[t][:].indirect(l3[:, h * HALF // 16 : (h + 1) * HALF // 16]), values, COPY)

        def pick(t, h, picks, hid):
            ent = slice(h * HALF // 16, (h + 1) * HALF // 16)
            nc.scalar.activation(picks[t][:], boards[t][:].indirect(l4[:, ent]), COPY, scale=sa_t[:, t : t + 1])
            pairs = picks[t][:].rearrange("p (o two) -> p o two", two=2)
            nc.vector.tensor_tensor(hid[:, :, t], pairs[:, :, 0], pairs[:, :, 1], ALU.max)

        def make_hidden(gathered, h, ts, copy):
            name = "a%d_%d" % (h, ts[0])
            bank = hidden(gathered, ts, name + "_bank")
            values = tile(name, [P, len(ts), HALF], F32)
            copy(values[:], bank[:])
            return values

        deal_scales(0)
        gathered = gather_half(0)
        a00 = make_hidden(gathered, 0, [0], nc.scalar.copy)
        put(0, 0, a00[:, 0, :])
        deal_scales(1)
        a01 = make_hidden(gathered, 0, [1], nc.vector.tensor_copy)
        put(1, 0, a01[:, 0, :])
        deal_scales(2)
        deal_scales(3)
        a02 = make_hidden(gathered, 0, [2, 3], nc.vector.tensor_copy)
        put(2, 0, a02[:, 0, :])
        put(3, 0, a02[:, 1, :])
        gathered = gather_half(1)
        a10 = make_hidden(gathered, 1, [0], nc.vector.tensor_copy)
        a11 = make_hidden(gathered, 1, [1], nc.vector.tensor_copy)
        a12 = make_hidden(gathered, 1, [2, 3], nc.vector.tensor_copy)

        xs_g = tile("xs_g", [P, O], U32, tag="xo_g")
        xs_gs = tile("xs_gs", [P, O], U8, tag="xo_gs")
        nc.vector.tensor_copy(xs_gs[:], xt_plane[:].indirect(l5[:]))
        nc.vector.tensor_copy(xs_g[:], xt_tab[:].indirect(l5[:]))
        x_bank = psum.tile([P, 2, O], F32, name="x_bank")
        y_bank = psum.tile([P, 2, O], F32, name="y_bank")
        for u in range(2):
            nc.tensor.matmul_mx(
                x_bank[:, u, :], lhsT=ws_tab[:, 256 * u : 256 * (u + 1)].bitcast(E2M1), lhsT_scale=ws_plane[:, P * u : P * (u + 1)],
                rhs=xs_g[:].bitcast(E5M2), rhs_scale=xs_gs[:], start=(u == 0), stop=False,
            )
        page_a = [tile("page_a%d" % u, [P, E], F32, tag=("xo_tab", "xo_plane")[u]) for u in range(2)]
        page_b = [tile("page_b%d" % u, [P, E], F32, tag=("xt_tab", "xt_plane")[u]) for u in range(2)]
        for page in page_a + page_b:
            nc.vector.memset(page[:], 0.0)

        picks0 = [tile("picks0_%d" % t, [P, HALF], F32) for t in range(PACK)]
        hid0 = tile("hid0", [P, O // 2, PACK], BF16)
        put(0, 1, a10[:, 0, :])
        put(1, 1, a11[:, 0, :])
        pick(0, 0, picks0, hid0)
        put(2, 1, a12[:, 0, :])
        pick(1, 0, picks0, hid0)
        put(3, 1, a12[:, 1, :])
        pick(2, 0, picks0, hid0)
        pick(3, 0, picks0, hid0)

        def pool_product(h, hid, bank, start):
            cols = slice(h * O // 2, (h + 1) * O // 2)
            nc.vector.quantize_mx(hid_q[:, cols].bitcast(E4M3), hid_s[:, cols], hid[:].rearrange("p o t -> p (o t)"))
            for u in range(2):
                nc.tensor.matmul_mx(
                    bank[:, u, :], lhsT=wb_tab[:, 256 * u : 256 * (u + 1)].bitcast(E2M1), lhsT_scale=wb_plane[:, P * u : P * (u + 1)],
                    rhs=hid_q[:].bitcast(E4M3), rhs_scale=hid_s[:], start=start, stop=start or u == 1,
                )

        def place(engine, page, offsets, h, values):
            window = page[:].indirect(offsets[:, h * O // 32 : (h + 1) * O // 32])
            if engine == "scalar":
                nc.scalar.activation(window, values, COPY)
            else:
                nc.vector.tensor_copy(window, values)

        pool_product(0, hid0, x_bank, False)
        hid1 = tile("hid1", [P, O // 2, PACK], BF16, tag="hid0")
        picks1 = [tile("picks1_%d" % t, [P, HALF], F32, tag=("a1_2", "picks0_2", None, None)[t]) for t in range(PACK)]
        for t in (2, 3, 0, 1):
            pick(t, 1, picks1, hid1)
        x_sb = tile("x_sb", [P, 2, O], F32)
        nc.scalar.copy(x_sb[:], x_bank[:])
        pool_product(1, hid1, y_bank, True)
        for pages, offsets in ((page_a, l6), (page_b, l7)):
            for u in range(2):
                place("scalar", pages[u], offsets, 0, x_sb[:, u, 0 : O // 2])
        p_hi = tile("p_hi", [P, 2, O // 2], F32)
        nc.vector.tensor_tensor(p_hi[:], y_bank[:, :, O // 2 :], x_sb[:, :, O // 2 :], ALU.add)
        for u in range(2):
            place("vector", page_a[u], l6, 1, p_hi[:, u, :])
            place("scalar", page_b[u], l7, 1, p_hi[:, u, :])
        for u in range(2):
            y = tile("y%d" % u, [P, E], F32)
            pieces = 1 + u
            for k in range(pieces):
                cols = slice(k * E // pieces, (k + 1) * E // pieces)
                nc.vector.tensor_tensor(y[:, cols], page_a[u][:, cols], page_b[u][:, cols], ALU.add)
                (nc.sync, nc.scalar)[k].dma_start(out[P * u : P * (u + 1), cols], y[:, cols])
